import numpy as np
import ml_dtypes


def mxq(x, axis, fmt="e4m3"):
    dtype, down = {"e4m3": (ml_dtypes.float8_e4m3fn, 7), "e5m2": (ml_dtypes.float8_e5m2, 14)}[fmt]
    v = np.moveaxis(np.asarray(x, np.float32).astype(ml_dtypes.bfloat16).astype(np.float64), axis, -1)
    blocks = v.reshape(v.shape[:-1] + (-1, 32))
    amax = np.abs(blocks).max(-1, keepdims=True)
    byte = np.maximum(np.where(amax > 0, np.frexp(amax)[1] - 1 + 127, 0) - down, 1)
    scale = np.exp2(byte - 127.0)
    codes = (blocks / scale).astype(np.float32).astype(dtype).astype(np.float64)
    return np.moveaxis((codes * scale).reshape(v.shape), -1, axis)


WIDE = False


def mx_kscale(k):
    if not WIDE:
        return np.ones(k)
    levels = np.array([10, -10, 5, -5, 0])
    if k % 512:
        return np.exp2(np.random.permutation(np.resize(levels, k // 32))).repeat(32)
    a = np.empty((k // 512, 16))
    for p in range(k // 512):
        a[p, :8] = np.random.permutation(np.resize(levels, 8))
        for g in range(8):
            far = levels[np.abs(levels - a[p, g]) >= 10]
            a[p, g + 8] = far[np.random.randint(len(far))]
    return np.exp2(a.ravel()).repeat(32)


BF16 = ml_dtypes.bfloat16


def bf(x):
    return np.asarray(x, np.float32).astype(BF16)


def f64(x):
    return np.asarray(x).astype(np.float64)


E2M1 = np.array([0.0, 0.5, 1.0, 1.5, 2.0, 3.0, 4.0, 6.0, -0.0, -0.5, -1.0, -1.5, -2.0, -3.0, -4.0, -6.0])


def pack_weight(w, fmt):
    k, n = w.shape
    w = f64(bf(w)).reshape(k // 32, 32, n)
    amax = np.abs(w).max(1)
    if fmt == "e4m3":
        byte = np.frexp(amax)[1] - 1 + 127 - 7
    else:
        mant, ex = np.frexp(amax / 6.0)
        byte = np.where(mant > 0.5, ex, ex - 1) + 127
    byte = np.clip(np.where(amax > 0, byte, 1), 1, 254)
    scaled = (w * np.exp2(127.0 - byte)[:, None, :]).reshape(k, n).astype(np.float32)
    by_word = np.ascontiguousarray(scaled.reshape(k // 512, 128, 4, n).transpose(0, 1, 3, 2))
    if fmt == "e4m3":
        words = by_word.astype(ml_dtypes.float8_e4m3fn).view(np.uint8)
    else:
        c = by_word.astype(ml_dtypes.float4_e2m1fn).view(np.uint8) & 0xF
        words = c[..., 0::2] | (c[..., 1::2] << 4)
    return np.ascontiguousarray(words), np.ascontiguousarray(byte.astype(np.uint8).reshape(k // 512, 16, n))


def unpack_weight(words, scales, fmt):
    g, p, n, _ = words.shape
    if fmt == "e4m3":
        vals = np.ascontiguousarray(words).view(ml_dtypes.float8_e4m3fn).astype(np.float64)
    else:
        nib = np.empty((g, p, n, 4), np.uint8)
        nib[..., 0::2] = words & 0xF
        nib[..., 1::2] = words >> 4
        vals = E2M1[nib]
    vals = vals * np.repeat(np.exp2(scales.astype(np.float64) - 127.0), 8, axis=1)[..., None]
    return vals.transpose(0, 1, 3, 2).reshape(g * 512, n)
def pack4(w):
    words, scales = pack_weight(w, "e2m1")
    return words.reshape(words.shape[0], 128, -1), scales


def unpack4(words, scales):
    return unpack_weight(words.reshape(words.shape[0], 128, -1, 2), scales, "e2m1")


ANT, SLOT, DEV, LOAD = 1024, 2048, 1536, 512


def setup_inputs():
    s = mx_kscale(ANT)
    t = mx_kscale(DEV)
    beam = np.random.standard_normal((ANT, SLOT)) * s[:, None]
    chan = 1.5 * np.random.standard_normal((ANT, DEV)) / np.sqrt(ANT) / s[:, None]
    alloc = np.random.standard_normal((DEV, LOAD)) / np.sqrt(DEV) / t[:, None]
    beam_words, beam_scales = pack4(beam)
    chan_words, chan_scales = pack4(chan)
    alloc_words, alloc_scales = pack_weight(alloc, "e4m3")
    return {"beam_words": beam_words, "beam_scales": beam_scales,
            "chan_words": chan_words, "chan_scales": chan_scales,
            "turn_on": bf(1.5 + 0.3 * np.random.standard_normal(DEV)),
            "sat": bf((1.0 + 0.1 * np.random.standard_normal(DEV)) * t),
            "alloc_words": alloc_words, "alloc_scales": alloc_scales}


def reference(beam_words, beam_scales, chan_words, chan_scales, turn_on, sat, alloc_words, alloc_scales):
    beam = unpack4(beam_words, beam_scales)
    chan = unpack4(chan_words, chan_scales)
    amp = beam.T @ chan
    harvest = f64(sat) / (1.0 + np.exp(f64(turn_on) - np.square(amp)))
    alloc = unpack_weight(alloc_words, alloc_scales, "e4m3")
    return mxq(harvest, 1, "e4m3") @ alloc

@@ -1,0 +1,319 @@
+from contextlib import ExitStack
+
+import concourse.mybir as mybir
+
+F32 = mybir.dt.float32
+BF16 = mybir.dt.bfloat16
+I32 = mybir.dt.int32
+U32 = mybir.dt.uint32
+U8 = mybir.dt.uint8
+FP8X4 = mybir.dt.float8_e4m3fn_x4
+FP4X4 = mybir.dt.float4_e2m1fn_x4
+ACT = mybir.ActivationFunctionType
+ALU = mybir.AluOpType
+
+ANT, SLOT, DEV, LOAD = 1024, 2048, 1536, 512
+FLOPS = 2 * ANT * SLOT * DEV + 2 * SLOT * DEV * LOAD
+
+P = 128
+K_PASS = 512
+KP = ANT // K_PASS
+NG = DEV // K_PASS
+C = 512
+NC = SLOT // C
+NT = 4
+
+LEAD = 5
+VSQ = {2, 3}
+
+
+def tile_wireless_power_allocation_s4_kernel(
+    tc, beam_words, beam_scales, chan_words, chan_scales, turn_on, sat, alloc_words, alloc_scales, out
+):
+    nc = tc.nc
+    n_units = NC * NG
+    n_steps = n_units * NT
+    last = n_units - 1
+
+    with ExitStack() as ctx:
+        keep = ctx.enter_context(tc.tile_pool(name="keep", bufs=1))
+        sqp = ctx.enter_context(tc.tile_pool(name="sqp", bufs=4))
+        sigp = ctx.enter_context(tc.tile_pool(name="sigp", bufs=3))
+        hbp = ctx.enter_context(tc.tile_pool(name="hbp", bufs=3))
+        qp = ctx.enter_context(tc.tile_pool(name="qp", bufs=6))
+        op = ctx.enter_context(tc.tile_pool(name="op", bufs=4))
+        amps = ctx.enter_context(tc.psum_pool(name="amps", bufs=6))
+        outs = ctx.enter_context(tc.psum_pool(name="outs", bufs=2))
+        ctx.enter_context(tc.manual_schedule())
+
+        chan_raw0 = keep.tile([P, KP, 1024], U8, name="chan_raw0", align_bytes=64)
+        chan_raw12 = keep.tile([P, KP, 2048], U8, name="chan_raw12", align_bytes=64)
+        chan_sraw0 = keep.tile([P, KP, 512], U8, name="chan_sraw0", align_bytes=64)
+        chan_sraw12 = keep.tile([P, KP, 1024], U8, name="chan_sraw12", align_bytes=64)
+        chan_c = [keep.tile([P, NT, KP, 256], U8, name=f"chan_c{g}", align_bytes=64) for g in range(NG)]
+        chan_s = [keep.tile([P, NT, KP, P], U8, name=f"chan_s{g}", align_bytes=64) for g in range(NG)]
+        beam_c = [keep.tile([P, KP, 2 * C], U8, name=f"beam_c{c}", align_bytes=64) for c in range(NC)]
+        beam_s0 = keep.tile([P, KP, C], U8, name="beam_s0", align_bytes=64)
+        beam_s123 = keep.tile([P, KP, 3 * C], U8, name="beam_s123", align_bytes=64)
+        alloc_c = keep.tile([P, NG, 4 * LOAD], U8, name="alloc_c", align_bytes=64)
+        alloc_s = keep.tile([P, NG, LOAD], U8, name="alloc_s", align_bytes=64)
+        ton_b = keep.tile([P, NG, NT], BF16, name="ton_b")
+        sat_b = keep.tile([P, NG, NT], BF16, name="sat_b")
+        neg_ton = keep.tile([P, NG * NT], F32, name="neg_ton")
+        sat_f = keep.tile([P, NG * NT], F32, name="sat_f")
+        dummy = keep.tile([P, 1], F32, name="dummy")
+        dummy2 = keep.tile([P, 1], F32, name="dummy2")
+
+        nc.vector.memset(chan_sraw0[:].bitcast(I32), 0)
+        nc.vector.memset(beam_s0[:].bitcast(I32), 0)
+        nc.gpsimd.memset(dummy[:], 0.0)
+        nc.gpsimd.dma_start(out=ton_b[:], in_=turn_on.rearrange("(g p t) -> p g t", g=NG, t=NT))
+        nc.gpsimd.dma_start(out=sat_b[:], in_=sat.rearrange("(g p t) -> p g t", g=NG, t=NT))
+        nc.gpsimd.memset(chan_sraw12[:].bitcast(I32), 0)
+        nc.gpsimd.memset(beam_s123[:].bitcast(I32), 0)
+        nc.gpsimd.memset(alloc_s[:].bitcast(I32), 0)
+
+        cw = chan_words.bitcast(I32).rearrange("k p n -> p k n")
+        bw = beam_words.bitcast(I32).rearrange("k p n -> p k n")
+        cs = chan_scales.bitcast(I32).rearrange("k r n -> r k n")
+        bs = beam_scales.bitcast(I32).rearrange("k r n -> r k n")
+        als = alloc_scales.bitcast(I32).rearrange("k r n -> r k n")
+
+        def load_scales(eng, tile, src, c0, c1):
+            view = tile[:].bitcast(I32)
+            for q in range(4):
+                eng.dma_start(out=view[32 * q : 32 * q + 4], in_=src[4 * q : 4 * q + 4, :, c0:c1])
+
+        nc.sync.dma_start(out=chan_raw0[:].bitcast(I32), in_=cw[:, :, 0:256])
+        nc.sync.dma_start(out=beam_c[0][:].bitcast(I32), in_=bw[:, :, 0:256])
+        load_scales(nc.scalar, chan_sraw0, cs, 0, 128)
+        load_scales(nc.scalar, beam_s0, bs, 0, 128)
+        nc.scalar.activation(out=dummy2[:], in_=dummy[:], func=ACT.Sigmoid)
+        load_scales(nc.sync, chan_sraw12, cs, 128, 384)
+        nc.sync.dma_start(out=chan_raw12[:].bitcast(I32), in_=cw[:, :, 256:768])
+        load_scales(nc.sync, beam_s123, bs, 128, 512)
+        nc.sync.dma_start(out=beam_c[1][:].bitcast(I32), in_=bw[:, :, 256:512])
+        nc.sync.dma_start(
+            out=alloc_c[:].bitcast(I32),
+            in_=alloc_words.rearrange("g p n t -> g p (n t)").bitcast(I32).rearrange("g p n -> p g n"),
+        )
+        load_scales(nc.sync, alloc_s, als, 0, 128)
+        for c in (2, 3):
+            nc.sync.dma_start(out=beam_c[c][:].bitcast(I32), in_=bw[:, :, 256 * c : 256 * (c + 1)])
+        nc.gpsimd.tensor_scalar(
+            out=neg_ton[:], in0=ton_b[:].rearrange("p g t -> p (g t)"), scalar1=-1.0, scalar2=0.0, op0=ALU.mult, op1=ALU.add
+        )
+        nc.gpsimd.tensor_copy(out=sat_f[:], in_=sat_b[:].rearrange("p g t -> p (g t)"))
+
+        def permute_first(t):
+            nc.vector.tensor_copy(
+                out=chan_c[0][:].rearrange("p t k (m b) -> p t k m b", b=2)[:, t],
+                in_=chan_raw0[:].rearrange("p k (m t b) -> p t k m b", t=NT, b=2)[:, t],
+            )
+            nc.vector.tensor_copy(
+                out=chan_s[0][:, t], in_=chan_sraw0[:].rearrange("p k (m t) -> p t k m", t=NT)[:, t]
+            )
+
+        def permute_codes(g, k):
+            src = chan_raw12[:, :, 1024 * (g - 1) : 1024 * g]
+            nc.vector.tensor_copy(
+                out=chan_c[g][:].rearrange("p t k (m b) -> p k t m b", b=2)[:, k],
+                in_=src.rearrange("p k (m t b) -> p k t m b", t=NT, b=2)[:, k],
+            )
+
+        def permute_scales(g):
+            src = chan_sraw12[:, :, 512 * (g - 1) : 512 * g]
+            nc.vector.tensor_copy(out=chan_s[g][:], in_=src.rearrange("p k (m t) -> p t k m", t=NT))
+
+        amp, sq, raw, sig, hb, codes, scales, acc = {}, {}, {}, {}, {}, {}, {}, {}
+
+        def mm1(k):
+            u, t = divmod(k, NT)
+            c, g = divmod(u, NG)
+            a = amps.tile([P, C], F32, name="amp")
+            amp[k] = a
+            for kk in range(KP):
+                if c == 0:
+                    rs = beam_s0[:, kk, :]
+                else:
+                    rs = beam_s123[:, kk, C * (c - 1) : C * c]
+                nc.tensor.matmul_mx(
+                    out=a[:],
+                    lhsT=chan_c[g][:, t, kk, :].bitcast(FP4X4),
+                    lhsT_scale=chan_s[g][:, t, kk, :],
+                    rhs=beam_c[c][:, kk, :].bitcast(FP4X4),
+                    rhs_scale=rs,
+                    start=(kk == 0),
+                    stop=(kk == KP - 1),
+                )
+
+        def square_s(k):
+            s = sqp.tile([P, C], F32, name="sq")
+            sq[k] = s
+            nc.scalar.activation(out=s[:], in_=amp[k][:], func=ACT.Square)
+
+        def square_v_copy(k):
+            r = sqp.tile([P, C], F32, name="raw")
+            raw[k] = r
+            nc.vector.tensor_copy(out=r[:], in_=amp[k][:])
+
+        def square_v_mult(k):
+            s = sqp.tile([P, C], F32, name="sq")
+            sq[k] = s
+            nc.vector.tensor_tensor(out=s[:], in0=raw[k][:], in1=raw[k][:], op=ALU.mult)
+
+        def sigmoid(k, c0=0, c1=C):
+            u, t = divmod(k, NT)
+            g = u % NG
+            if u not in sig:
+                s = sigp.tile([P, NT, C], F32, name="sig")
+                sig[u] = s
+            nc.scalar.activation(
+                out=sig[u][:, t, c0:c1],
+                in_=sq[k][:, c0:c1],
+                func=ACT.Sigmoid,
+                bias=neg_ton[:, NT * g + t : NT * g + t + 1],
+            )
+
+        def scale_by_sat(u, c0, c1):
+            g = u % NG
+            h = hbp.tile([P, 1024], BF16, name="hb", align_bytes=64)
+            hb[u, c0] = h
+            n = c1 - c0
+            nc.vector.tensor_tensor(
+                out=h[:, 0 : NT * n].rearrange("p (c i t) -> p c t i", i=4, t=NT),
+                in0=sig[u][:, :, c0:c1].rearrange("p t (c i) -> p c t i", i=4),
+                in1=sat_f[:, NT * g : NT * (g + 1)].unsqueeze(1).unsqueeze(3).broadcast_to([P, n // 4, NT, 4]),
+                op=ALU.mult,
+            )
+
+        def quantize(u, c0, c1):
+            if u not in codes:
+                qc = qp.tile([P, C], U32, name="qc", align_bytes=64)
+                qs = qp.tile([P, C], U8, name="qs", align_bytes=64)
+                codes[u] = qc
+                scales[u] = qs
+            nc.vector.quantize_mx(
+                out=codes[u][:, c0:c1].bitcast(FP8X4),
+                scales=scales[u][:, c0:c1],
+                in_=hb[u, c0][:, 0 : NT * (c1 - c0)],
+            )
+
+        def mm2(c, st, g0, g1, pool):
+            if g0 == 0:
+                if pool == "outs":
+                    a = outs.tile([P, LOAD], F32, name="acc")
+                else:
+                    a = amps.tile([P, LOAD], F32, name="amp")
+                acc[c, st] = a
+            for g in range(g0, g1):
+                u = NG * c + g
+                nc.tensor.matmul_mx(
+                    out=acc[c, st][:],
+                    lhsT=codes[u][:, P * st : P * (st + 1)].bitcast(FP8X4),
+                    lhsT_scale=scales[u][:, P * st : P * (st + 1)],
+                    rhs=alloc_c[:, g, :].bitcast(FP8X4),
+                    rhs_scale=alloc_s[:, g, :],
+                    start=(g == 0),
+                    stop=(g == NG - 1),
+                )
+
+        def finish(c, st, eng):
+            o = op.tile([P, LOAD], F32, name="o")
+            if eng == "v":
+                nc.vector.tensor_copy(out=o[:], in_=acc[c, st][:])
+            else:
+                nc.scalar.copy(out=o[:], in_=acc[c, st][:])
+            row = C * c + P * st
+            nc.sync.dma_start(out=out[row : row + P, :], in_=o[:])
+
+        def square(k):
+            if k < n_steps and k not in VSQ:
+                square_s(k)
+
+        for t in range(NT):
+            permute_first(t)
+            mm1(t)
+        square_v_copy(2)
+        permute_codes(1, 0)
+        square_v_mult(2)
+        square_v_copy(3)
+        permute_codes(1, 1)
+        square_v_mult(3)
+        permute_scales(1)
+        mm1(4)
+        square(0)
+        v_early = [lambda: permute_codes(2, 0), lambda: permute_codes(2, 1), lambda: permute_scales(2)]
+
+        for k in range(n_steps - NT):
+            u, j = divmod(k, NT)
+            c, g = divmod(u, NG)
+            if k < 3:
+                v_early[k]()
+            if k + LEAD < n_steps:
+                mm1(k + LEAD)
+            square(k + 1)
+            sigmoid(k)
+            pu = u - 1
+            done = u >= 1 and pu % NG == NG - 1
+            pc = pu // NG
+            if u >= 1:
+                if j == 0:
+                    scale_by_sat(pu, 0, 256)
+                if j == 1:
+                    scale_by_sat(pu, 256, 512)
+                    quantize(pu, 0, 256)
+                    if done:
+                        mm2(pc, 0, 0, NG, "outs")
+                        mm2(pc, 1, 0, NG, "outs")
+                if j == 2:
+                    quantize(pu, 256, 512)
+                    if done:
+                        finish(pc, 0, "v")
+                        mm2(pc, 2, 0, NG, "outs")
+                if j == 3:
+                    if done:
+                        finish(pc, 1, "v")
+                        mm2(pc, 3, 0, NG, "outs")
+            if u >= 2 and (u - 2) % NG == NG - 1:
+                if j == 0:
+                    finish((u - 2) // NG, 2, "v")
+                if j == 1:
+                    finish((u - 2) // NG, 3, "v")
+            if k + 3 in VSQ and k + 3 >= NT:
+                square_v_copy(k + 3)
+            if k + 2 in VSQ and k + 2 >= NT:
+                square_v_mult(k + 2)
+
+        k0 = n_steps - NT
+        lc = NC - 1
+        segs = [(0, 256), (256, 384), (384, 512)]
+        pu = last - 1
+        square(k0 + 1)
+        square(k0 + 2)
+        square(k0 + 3)
+        scale_by_sat(pu, 0, 256)
+        scale_by_sat(pu, 256, 512)
+        quantize(pu, 0, 256)
+        quantize(pu, 256, 512)
+        for i, (c0, c1) in enumerate(segs):
+            for t in range(NT):
+                sigmoid(k0 + t, c0, c1)
+        mm2(lc, 0, 0, NG - 1, "outs")
+        mm2(lc, 1, 0, NG - 1, "outs")
+        mm2(lc, 2, 0, NG - 1, "amps")
+        mm2(lc, 3, 0, NG - 1, "amps")
+        scale_by_sat(last, 0, 256)
+        scale_by_sat(last, 256, 384)
+        quantize(last, 0, 256)
+        mm2(lc, 0, NG - 1, NG, "outs")
+        mm2(lc, 1, NG - 1, NG, "outs")
+        finish(lc, 0, "s")
+        finish(lc, 1, "s")
+        scale_by_sat(last, 384, 512)
+        quantize(last, 256, 384)
+        mm2(lc, 2, NG - 1, NG, "amps")
+        finish(lc, 2, "s")
+        quantize(last, 384, 512)
+        mm2(lc, 3, NG - 1, NG, "amps")
+        finish(lc, 3, "v")

@@ -40,7 +40,7 @@ def tile_wireless_power_allocation_s4_kernel(
         sqp = ctx.enter_context(tc.tile_pool(name="sqp", bufs=4))
         sigp = ctx.enter_context(tc.tile_pool(name="sigp", bufs=3))
         hbp = ctx.enter_context(tc.tile_pool(name="hbp", bufs=3))
-        qp = ctx.enter_context(tc.tile_pool(name="qp", bufs=6))
+        qp = ctx.enter_context(tc.tile_pool(name="qp", bufs=8))
         op = ctx.enter_context(tc.tile_pool(name="op", bufs=4))
         amps = ctx.enter_context(tc.psum_pool(name="amps", bufs=6))
         outs = ctx.enter_context(tc.psum_pool(name="outs", bufs=2))
@@ -66,12 +66,10 @@ def tile_wireless_power_allocation_s4_kernel(
 
         nc.vector.memset(chan_sraw0[:].bitcast(I32), 0)
         nc.vector.memset(beam_s0[:].bitcast(I32), 0)
-        nc.gpsimd.memset(dummy[:], 0.0)
-        nc.gpsimd.dma_start(out=ton_b[:], in_=turn_on.rearrange("(g p t) -> p g t", g=NG, t=NT))
-        nc.gpsimd.dma_start(out=sat_b[:], in_=sat.rearrange("(g p t) -> p g t", g=NG, t=NT))
-        nc.gpsimd.memset(chan_sraw12[:].bitcast(I32), 0)
-        nc.gpsimd.memset(beam_s123[:].bitcast(I32), 0)
-        nc.gpsimd.memset(alloc_s[:].bitcast(I32), 0)
+        nc.vector.memset(dummy[:], 0.0)
+        nc.vector.memset(beam_s123[:].bitcast(I32), 0)
+        nc.vector.memset(chan_sraw12[:].bitcast(I32), 0)
+        nc.vector.memset(alloc_s[:].bitcast(I32), 0)
 
         cw = chan_words.bitcast(I32).rearrange("k p n -> p k n")
         bw = beam_words.bitcast(I32).rearrange("k p n -> p k n")
@@ -79,27 +77,33 @@ def tile_wireless_power_allocation_s4_kernel(
         bs = beam_scales.bitcast(I32).rearrange("k r n -> r k n")
         als = alloc_scales.bitcast(I32).rearrange("k r n -> r k n")
 
-        def load_scales(eng, tile, src, c0, c1):
+        def load_scales(eng, tile, src, c0, c1, quarters=(0, 1, 2, 3)):
             view = tile[:].bitcast(I32)
-            for q in range(4):
+            for q in quarters:
                 eng.dma_start(out=view[32 * q : 32 * q + 4], in_=src[4 * q : 4 * q + 4, :, c0:c1])
 
+        def load_beam(eng, c):
+            eng.dma_start(out=beam_c[c][:].bitcast(I32), in_=bw[:, :, 256 * c : 256 * (c + 1)])
+
+        load_beam(nc.gpsimd, 0)
         nc.sync.dma_start(out=chan_raw0[:].bitcast(I32), in_=cw[:, :, 0:256])
-        nc.sync.dma_start(out=beam_c[0][:].bitcast(I32), in_=bw[:, :, 0:256])
         load_scales(nc.scalar, chan_sraw0, cs, 0, 128)
-        load_scales(nc.scalar, beam_s0, bs, 0, 128)
+        load_scales(nc.sync, beam_s0, bs, 0, 128, (0, 1, 2))
+        load_scales(nc.gpsimd, beam_s0, bs, 0, 128, (3,))
+        nc.gpsimd.dma_start(out=ton_b[:], in_=turn_on.rearrange("(g p t) -> p g t", g=NG, t=NT))
+        nc.gpsimd.dma_start(out=sat_b[:], in_=sat.rearrange("(g p t) -> p g t", g=NG, t=NT))
         nc.scalar.activation(out=dummy2[:], in_=dummy[:], func=ACT.Sigmoid)
+        load_scales(nc.sync, beam_s123, bs, 128, 512)
+        load_beam(nc.sync, 1)
         load_scales(nc.sync, chan_sraw12, cs, 128, 384)
         nc.sync.dma_start(out=chan_raw12[:].bitcast(I32), in_=cw[:, :, 256:768])
-        load_scales(nc.sync, beam_s123, bs, 128, 512)
-        nc.sync.dma_start(out=beam_c[1][:].bitcast(I32), in_=bw[:, :, 256:512])
         nc.sync.dma_start(
             out=alloc_c[:].bitcast(I32),
             in_=alloc_words.rearrange("g p n t -> g p (n t)").bitcast(I32).rearrange("g p n -> p g n"),
         )
         load_scales(nc.sync, alloc_s, als, 0, 128)
-        for c in (2, 3):
-            nc.sync.dma_start(out=beam_c[c][:].bitcast(I32), in_=bw[:, :, 256 * c : 256 * (c + 1)])
+        load_beam(nc.sync, 2)
+        load_beam(nc.sync, 3)
         nc.gpsimd.tensor_scalar(
             out=neg_ton[:], in0=ton_b[:].rearrange("p g t -> p (g t)"), scalar1=-1.0, scalar2=0.0, op0=ALU.mult, op1=ALU.add
         )
@@ -125,11 +129,14 @@ def tile_wireless_power_allocation_s4_kernel(
             src = chan_sraw12[:, :, 512 * (g - 1) : 512 * g]
             nc.vector.tensor_copy(out=chan_s[g][:], in_=src.rearrange("p k (m t) -> p t k m", t=NT))
 
+        order = [(0, 0), (1, 0), (0, 1), (1, 1), (0, 2), (1, 2)] + [(c, g) for c in (2, 3) for g in range(NG)]
+        index = {cg: u for u, cg in enumerate(order)}
+        ends = {index[c, NG - 1]: c for c in range(NC)}
         amp, sq, raw, sig, hb, codes, scales, acc = {}, {}, {}, {}, {}, {}, {}, {}
 
         def mm1(k):
             u, t = divmod(k, NT)
-            c, g = divmod(u, NG)
+            c, g = order[u]
             a = amps.tile([P, C], F32, name="amp")
             amp[k] = a
             for kk in range(KP):
@@ -164,7 +171,7 @@ def tile_wireless_power_allocation_s4_kernel(
 
         def sigmoid(k, c0=0, c1=C):
             u, t = divmod(k, NT)
-            g = u % NG
+            g = order[u][1]
             if u not in sig:
                 s = sigp.tile([P, NT, C], F32, name="sig")
                 sig[u] = s
@@ -176,14 +183,14 @@ def tile_wireless_power_allocation_s4_kernel(
             )
 
         def scale_by_sat(u, c0, c1):
-            g = u % NG
+            g = order[u][1]
             h = hbp.tile([P, 1024], BF16, name="hb", align_bytes=64)
             hb[u, c0] = h
             n = c1 - c0
             nc.vector.tensor_tensor(
-                out=h[:, 0 : NT * n].rearrange("p (c i t) -> p c t i", i=4, t=NT),
-                in0=sig[u][:, :, c0:c1].rearrange("p t (c i) -> p c t i", i=4),
-                in1=sat_f[:, NT * g : NT * (g + 1)].unsqueeze(1).unsqueeze(3).broadcast_to([P, n // 4, NT, 4]),
+                out=h[:, 0 : NT * n].rearrange("p (c i t) -> p c t i", i=2, t=NT),
+                in0=sig[u][:, :, c0:c1].rearrange("p t (c i) -> p c t i", i=2),
+                in1=sat_f[:, NT * g : NT * (g + 1)].unsqueeze(1).unsqueeze(3).broadcast_to([P, n // 2, NT, 2]),
                 op=ALU.mult,
             )
 
@@ -207,7 +214,7 @@ def tile_wireless_power_allocation_s4_kernel(
                     a = amps.tile([P, LOAD], F32, name="amp")
                 acc[c, st] = a
             for g in range(g0, g1):
-                u = NG * c + g
+                u = index[c, g]
                 nc.tensor.matmul_mx(
                     out=acc[c, st][:],
                     lhsT=codes[u][:, P * st : P * (st + 1)].bitcast(FP8X4),
@@ -235,28 +242,31 @@ def tile_wireless_power_allocation_s4_kernel(
             permute_first(t)
             mm1(t)
         square_v_copy(2)
-        permute_codes(1, 0)
-        square_v_mult(2)
         square_v_copy(3)
-        permute_codes(1, 1)
+        square_v_mult(2)
         square_v_mult(3)
-        permute_scales(1)
         mm1(4)
         square(0)
-        v_early = [lambda: permute_codes(2, 0), lambda: permute_codes(2, 1), lambda: permute_scales(2)]
+        v_early = {
+            1: lambda: permute_codes(1, 0),
+            2: lambda: permute_codes(1, 1),
+            3: lambda: permute_scales(1),
+            6: lambda: permute_codes(2, 0),
+            7: lambda: permute_codes(2, 1),
+            10: lambda: permute_scales(2),
+        }
 
         for k in range(n_steps - NT):
             u, j = divmod(k, NT)
-            c, g = divmod(u, NG)
-            if k < 3:
+            if k in v_early:
                 v_early[k]()
             if k + LEAD < n_steps:
                 mm1(k + LEAD)
             square(k + 1)
             sigmoid(k)
             pu = u - 1
-            done = u >= 1 and pu % NG == NG - 1
-            pc = pu // NG
+            done = pu in ends
+            pc = ends[pu] if done else None
             if u >= 1:
                 if j == 0:
                     scale_by_sat(pu, 0, 256)
@@ -275,11 +285,11 @@ def tile_wireless_power_allocation_s4_kernel(
                     if done:
                         finish(pc, 1, "v")
                         mm2(pc, 3, 0, NG, "outs")
-            if u >= 2 and (u - 2) % NG == NG - 1:
+            if u - 2 in ends:
                 if j == 0:
-                    finish((u - 2) // NG, 2, "v")
+                    finish(ends[u - 2], 2, "v")
                 if j == 1:
-                    finish((u - 2) // NG, 3, "v")
+                    finish(ends[u - 2], 3, "v")
             if k + 3 in VSQ and k + 3 >= NT:
                 square_v_copy(k + 3)
             if k + 2 in VSQ and k + 2 >= NT:

@@ -1,6 +1,7 @@
 from contextlib import ExitStack
 
 import concourse.mybir as mybir
+from concourse.masks import make_identity
 
 F32 = mybir.dt.float32
 BF16 = mybir.dt.bfloat16
@@ -23,8 +24,13 @@ C = 512
 NC = SLOT // C
 NT = 4
 
-LEAD = 5
-VSQ = {2, 3}
+LEAD = 4
+VSQ = [2, 9, 14, 18, 20, 26, 35, 38, 44]
+GS = 160
+AMPS = 5
+FSL = [(0, 3), (0, 3), (1, 1), (1, 3)]
+SEGS = [(0, 256), (256, 384), (384, 512)]
+AHD = 3
 
 
 def tile_wireless_power_allocation_s4_kernel(
@@ -39,10 +45,11 @@ def tile_wireless_power_allocation_s4_kernel(
         keep = ctx.enter_context(tc.tile_pool(name="keep", bufs=1))
         sqp = ctx.enter_context(tc.tile_pool(name="sqp", bufs=4))
         sigp = ctx.enter_context(tc.tile_pool(name="sigp", bufs=3))
-        hbp = ctx.enter_context(tc.tile_pool(name="hbp", bufs=3))
+        hbp = ctx.enter_context(tc.tile_pool(name="hbp", bufs=2))
         qp = ctx.enter_context(tc.tile_pool(name="qp", bufs=8))
-        op = ctx.enter_context(tc.tile_pool(name="op", bufs=4))
-        amps = ctx.enter_context(tc.psum_pool(name="amps", bufs=6))
+        op = ctx.enter_context(tc.tile_pool(name="op", bufs=6))
+        amps = ctx.enter_context(tc.psum_pool(name="amps", bufs=AMPS))
+        satp = ctx.enter_context(tc.psum_pool(name="satp", bufs=1))
         outs = ctx.enter_context(tc.psum_pool(name="outs", bufs=2))
         ctx.enter_context(tc.manual_schedule())
 
@@ -60,13 +67,16 @@ def tile_wireless_power_allocation_s4_kernel(
         ton_b = keep.tile([P, NG, NT], BF16, name="ton_b")
         sat_b = keep.tile([P, NG, NT], BF16, name="sat_b")
         neg_ton = keep.tile([P, NG * NT], F32, name="neg_ton")
-        sat_f = keep.tile([P, NG * NT], F32, name="sat_f")
+        sat_w = keep.tile([P, P], F32, name="sat_w")
+        sat_t = keep.tile([P, P], F32, name="sat_t")
+        ident = keep.tile([P, P], F32, name="ident")
         dummy = keep.tile([P, 1], F32, name="dummy")
         dummy2 = keep.tile([P, 1], F32, name="dummy2")
 
         nc.vector.memset(chan_sraw0[:].bitcast(I32), 0)
         nc.vector.memset(beam_s0[:].bitcast(I32), 0)
         nc.vector.memset(dummy[:], 0.0)
+        nc.vector.memset(sat_w[:], 0.0)
         nc.vector.memset(beam_s123[:].bitcast(I32), 0)
         nc.vector.memset(chan_sraw12[:].bitcast(I32), 0)
         nc.vector.memset(alloc_s[:].bitcast(I32), 0)
@@ -104,10 +114,11 @@ def tile_wireless_power_allocation_s4_kernel(
         load_scales(nc.sync, alloc_s, als, 0, 128)
         load_beam(nc.sync, 2)
         load_beam(nc.sync, 3)
+        make_identity(nc, ident[:])
         nc.gpsimd.tensor_scalar(
             out=neg_ton[:], in0=ton_b[:].rearrange("p g t -> p (g t)"), scalar1=-1.0, scalar2=0.0, op0=ALU.mult, op1=ALU.add
         )
-        nc.gpsimd.tensor_copy(out=sat_f[:], in_=sat_b[:].rearrange("p g t -> p (g t)"))
+        nc.gpsimd.tensor_copy(out=sat_w[:, 0 : NG * NT], in_=sat_b[:].rearrange("p g t -> p (g t)"))
 
         def permute_first(t):
             nc.vector.tensor_copy(
@@ -167,7 +178,7 @@ def tile_wireless_power_allocation_s4_kernel(
         def square_v_mult(k):
             s = sqp.tile([P, C], F32, name="sq")
             sq[k] = s
-            nc.vector.tensor_tensor(out=s[:], in0=raw[k][:], in1=raw[k][:], op=ALU.mult)
+            nc.vector.tensor_tensor(out=s[:], in0=amp[k][:], in1=raw[k][:], op=ALU.mult)
 
         def sigmoid(k, c0=0, c1=C):
             u, t = divmod(k, NT)
@@ -182,17 +193,22 @@ def tile_wireless_power_allocation_s4_kernel(
                 bias=neg_ton[:, NT * g + t : NT * g + t + 1],
             )
 
-        def scale_by_sat(u, c0, c1):
+        def scale_part(eng, u, h, base, c0, c1, factors):
             g = order[u][1]
-            h = hbp.tile([P, 1024], BF16, name="hb", align_bytes=64)
-            hb[u, c0] = h
             n = c1 - c0
-            nc.vector.tensor_tensor(
-                out=h[:, 0 : NT * n].rearrange("p (c i t) -> p c t i", i=2, t=NT),
+            eng.tensor_tensor(
+                out=h[:, NT * (c0 - base) : NT * (c1 - base)].rearrange("p (c i t) -> p c t i", i=2, t=NT),
                 in0=sig[u][:, :, c0:c1].rearrange("p t (c i) -> p c t i", i=2),
-                in1=sat_f[:, NT * g : NT * (g + 1)].unsqueeze(1).unsqueeze(3).broadcast_to([P, n // 2, NT, 2]),
+                in1=factors[:, NT * g : NT * (g + 1)].unsqueeze(1).unsqueeze(3).broadcast_to([P, n // 2, NT, 2]),
                 op=ALU.mult,
             )
+
+        def scale_by_sat(u, c0, c1, share=0):
+            h = hbp.tile([P, 4 * C], BF16, name="hb", align_bytes=64)
+            hb[u, c0] = h
+            if share:
+                scale_part(nc.gpsimd, u, h, c0, c1 - share, c1, sat_w)
+            scale_part(nc.vector, u, h, c0, c0, c1 - share, sat_ps)
 
         def quantize(u, c0, c1):
             if u not in codes:
@@ -206,33 +222,34 @@ def tile_wireless_power_allocation_s4_kernel(
                 in_=hb[u, c0][:, 0 : NT * (c1 - c0)],
             )
 
-        def mm2(c, st, g0, g1, pool):
-            if g0 == 0:
-                if pool == "outs":
-                    a = outs.tile([P, LOAD], F32, name="acc")
-                else:
-                    a = amps.tile([P, LOAD], F32, name="amp")
-                acc[c, st] = a
+        def mm2(c, st, g0, g1, a, n0=0, n1=LOAD):
             for g in range(g0, g1):
                 u = index[c, g]
                 nc.tensor.matmul_mx(
-                    out=acc[c, st][:],
+                    out=a[:, 0 : n1 - n0],
                     lhsT=codes[u][:, P * st : P * (st + 1)].bitcast(FP8X4),
                     lhsT_scale=scales[u][:, P * st : P * (st + 1)],
-                    rhs=alloc_c[:, g, :].bitcast(FP8X4),
-                    rhs_scale=alloc_s[:, g, :],
+                    rhs=alloc_c[:, g, 4 * n0 : 4 * n1].bitcast(FP8X4),
+                    rhs_scale=alloc_s[:, g, n0:n1],
                     start=(g == 0),
                     stop=(g == NG - 1),
                 )
 
-        def finish(c, st, eng):
+        def mm2_all(c, st):
+            a = outs.tile([P, LOAD], F32, name="acc")
+            acc[c, st] = a
+            mm2(c, st, 0, NG, a)
+
+        def finish(c, st, eng, a=None, n0=0, n1=LOAD, queue=None):
+            a = acc[c, st] if a is None else a
             o = op.tile([P, LOAD], F32, name="o")
+            w = n1 - n0
             if eng == "v":
-                nc.vector.tensor_copy(out=o[:], in_=acc[c, st][:])
+                nc.vector.tensor_copy(out=o[:, 0:w], in_=a[:, 0:w])
             else:
-                nc.scalar.copy(out=o[:], in_=acc[c, st][:])
+                nc.scalar.copy(out=o[:, 0:w], in_=a[:, 0:w])
             row = C * c + P * st
-            nc.sync.dma_start(out=out[row : row + P, :], in_=o[:])
+            (queue or nc.sync).dma_start(out=out[row : row + P, n0:n1], in_=o[:, 0:w])
 
         def square(k):
             if k < n_steps and k not in VSQ:
@@ -241,12 +258,18 @@ def tile_wireless_power_allocation_s4_kernel(
         for t in range(NT):
             permute_first(t)
             mm1(t)
-        square_v_copy(2)
-        square_v_copy(3)
-        square_v_mult(2)
-        square_v_mult(3)
-        mm1(4)
+        for k in range(NT):
+            if k in VSQ:
+                square_v_copy(k)
+        for k in range(NT):
+            if k in VSQ:
+                square_v_mult(k)
         square(0)
+        sat_tp = outs.tile([P, LOAD], F32, name="acc")
+        sat_ps = satp.tile([P, LOAD], F32, name="sat_ps")
+        nc.tensor.transpose(sat_tp[:, 0:P], sat_w[:], ident[:])
+        nc.vector.tensor_copy(out=sat_t[:], in_=sat_tp[:, 0:P])
+        nc.tensor.transpose(sat_ps[:, 0:P], sat_t[:], ident[:])
         v_early = {
             1: lambda: permute_codes(1, 0),
             2: lambda: permute_codes(1, 1),
@@ -255,7 +278,7 @@ def tile_wireless_power_allocation_s4_kernel(
             7: lambda: permute_codes(2, 1),
             10: lambda: permute_scales(2),
         }
-
+        fins = {}
         for k in range(n_steps - NT):
             u, j = divmod(k, NT)
             if k in v_early:
@@ -269,61 +292,56 @@ def tile_wireless_power_allocation_s4_kernel(
             pc = ends[pu] if done else None
             if u >= 1:
                 if j == 0:
-                    scale_by_sat(pu, 0, 256)
-                if j == 1:
-                    scale_by_sat(pu, 256, 512)
-                    quantize(pu, 0, 256)
-                    if done:
-                        mm2(pc, 0, 0, NG, "outs")
-                        mm2(pc, 1, 0, NG, "outs")
-                if j == 2:
-                    quantize(pu, 256, 512)
-                    if done:
-                        finish(pc, 0, "v")
-                        mm2(pc, 2, 0, NG, "outs")
-                if j == 3:
-                    if done:
-                        finish(pc, 1, "v")
-                        mm2(pc, 3, 0, NG, "outs")
-            if u - 2 in ends:
-                if j == 0:
-                    finish(ends[u - 2], 2, "v")
-                if j == 1:
-                    finish(ends[u - 2], 3, "v")
-            if k + 3 in VSQ and k + 3 >= NT:
-                square_v_copy(k + 3)
+                    scale_by_sat(pu, 0, 512, GS)
+            for f in fins.pop((u, j), []):
+                f()
+            if k + AHD in VSQ and k + AHD >= NT:
+                square_v_copy(k + AHD)
+            if u >= 1 and j == 2:
+                quantize(pu, 0, 512)
+                if done:
+                    mm2_all(pc, 0)
+                    mm2_all(pc, 1)
+                    for st, (du, fj) in enumerate(FSL):
+                        def fin(c=pc, st=st):
+                            finish(c, st, "v")
+                            if st < 2:
+                                mm2_all(c, st + 2)
+                        fins.setdefault((u + du, fj), []).append(fin)
             if k + 2 in VSQ and k + 2 >= NT:
                 square_v_mult(k + 2)
 
         k0 = n_steps - NT
         lc = NC - 1
-        segs = [(0, 256), (256, 384), (384, 512)]
+        segs = SEGS
         pu = last - 1
         square(k0 + 1)
         square(k0 + 2)
         square(k0 + 3)
-        scale_by_sat(pu, 0, 256)
-        scale_by_sat(pu, 256, 512)
-        quantize(pu, 0, 256)
-        quantize(pu, 256, 512)
-        for i, (c0, c1) in enumerate(segs):
+        scale_by_sat(pu, 0, 512, GS)
+        for key in sorted(fins):
+            for f in fins[key]:
+                f()
+        quantize(pu, 0, 512)
+        final = {}
+        for key in ("0", "1", "2", "3a", "3b"):
+            a = amps.tile([P, C], F32, name="amp")
+            final[key] = a
+        parts = [("0", 0, 0, 512), ("1", 1, 0, 512), ("2", 2, 0, 512), ("3a", 3, 0, 256), ("3b", 3, 256, 512)]
+        for key, s, n0, n1 in parts:
+            mm2(lc, s, 0, NG - 1, final[key], n0, n1)
+        for c0, c1 in segs:
             for t in range(NT):
                 sigmoid(k0 + t, c0, c1)
-        mm2(lc, 0, 0, NG - 1, "outs")
-        mm2(lc, 1, 0, NG - 1, "outs")
-        mm2(lc, 2, 0, NG - 1, "amps")
-        mm2(lc, 3, 0, NG - 1, "amps")
-        scale_by_sat(last, 0, 256)
-        scale_by_sat(last, 256, 384)
-        quantize(last, 0, 256)
-        mm2(lc, 0, NG - 1, NG, "outs")
-        mm2(lc, 1, NG - 1, NG, "outs")
-        finish(lc, 0, "s")
-        finish(lc, 1, "s")
-        scale_by_sat(last, 384, 512)
-        quantize(last, 256, 384)
-        mm2(lc, 2, NG - 1, NG, "amps")
-        finish(lc, 2, "s")
-        quantize(last, 384, 512)
-        mm2(lc, 3, NG - 1, NG, "amps")
-        finish(lc, 3, "v")
+        for i, (c0, c1) in enumerate(segs):
+            scale_by_sat(last, c0, c1)
+            if i > 0:
+                quantize(last, *segs[i - 1])
+        quantize(last, *segs[-1])
+        for key, s, n0, n1 in parts:
+            mm2(lc, s, NG - 1, NG, final[key], n0, n1)
+        finish(lc, 0, "s", final["0"])
+        finish(lc, 1, "s", final["1"])
+        finish(lc, 2, "v", final["2"])
+        finish(lc, 3, "s", final["3a"], 0, 256, nc.scalar)
+        finish(lc, 3, "v", final["3b"], 256, 512)

@@ -24,9 +24,13 @@ C = 512
 NC = SLOT // C
 NT = 4
 
-LEAD = 4
-VSQ = [2, 9, 14, 18, 20, 26, 35, 38, 44]
-GS = 160
+LEAD = 5
+VSQ = [3, 9, 13, 17, 21, 25, 29, 37, 41]
+CPJ = 1
+MUJ = 2
+SATK = 5
+GU = 1
+GS = 144
 AMPS = 5
 FSL = [(0, 3), (0, 3), (1, 1), (1, 3)]
 SEGS = [(0, 256), (256, 384), (384, 512)]
@@ -103,10 +107,10 @@ def tile_wireless_power_allocation_s4_kernel(
         nc.gpsimd.dma_start(out=ton_b[:], in_=turn_on.rearrange("(g p t) -> p g t", g=NG, t=NT))
         nc.gpsimd.dma_start(out=sat_b[:], in_=sat.rearrange("(g p t) -> p g t", g=NG, t=NT))
         nc.scalar.activation(out=dummy2[:], in_=dummy[:], func=ACT.Sigmoid)
+        nc.gpsimd.dma_start(out=chan_raw12[:].bitcast(I32), in_=cw[:, :, 256:768])
         load_scales(nc.sync, beam_s123, bs, 128, 512)
         load_beam(nc.sync, 1)
         load_scales(nc.sync, chan_sraw12, cs, 128, 384)
-        nc.sync.dma_start(out=chan_raw12[:].bitcast(I32), in_=cw[:, :, 256:768])
         nc.sync.dma_start(
             out=alloc_c[:].bitcast(I32),
             in_=alloc_words.rearrange("g p n t -> g p (n t)").bitcast(I32).rearrange("g p n -> p g n"),
@@ -114,11 +118,8 @@ def tile_wireless_power_allocation_s4_kernel(
         load_scales(nc.sync, alloc_s, als, 0, 128)
         load_beam(nc.sync, 2)
         load_beam(nc.sync, 3)
-        make_identity(nc, ident[:])
-        nc.gpsimd.tensor_scalar(
-            out=neg_ton[:], in0=ton_b[:].rearrange("p g t -> p (g t)"), scalar1=-1.0, scalar2=0.0, op0=ALU.mult, op1=ALU.add
-        )
         nc.gpsimd.tensor_copy(out=sat_w[:, 0 : NG * NT], in_=sat_b[:].rearrange("p g t -> p (g t)"))
+        make_identity(nc, ident[:])
 
         def permute_first(t):
             nc.vector.tensor_copy(
@@ -178,7 +179,7 @@ def tile_wireless_power_allocation_s4_kernel(
         def square_v_mult(k):
             s = sqp.tile([P, C], F32, name="sq")
             sq[k] = s
-            nc.vector.tensor_tensor(out=s[:], in0=amp[k][:], in1=raw[k][:], op=ALU.mult)
+            nc.vector.tensor_tensor(out=s[:], in0=raw[k][:], in1=raw[k][:], op=ALU.mult)
 
         def sigmoid(k, c0=0, c1=C):
             u, t = divmod(k, NT)
@@ -206,9 +207,11 @@ def tile_wireless_power_allocation_s4_kernel(
         def scale_by_sat(u, c0, c1, share=0):
             h = hbp.tile([P, 4 * C], BF16, name="hb", align_bytes=64)
             hb[u, c0] = h
+            if u < GU:
+                share = 0
             if share:
                 scale_part(nc.gpsimd, u, h, c0, c1 - share, c1, sat_w)
-            scale_part(nc.vector, u, h, c0, c0, c1 - share, sat_ps)
+            scale_part(nc.vector, u, h, c0, c0, c1 - share, sat_ps if u >= GU else sat_w)
 
         def quantize(u, c0, c1):
             if u not in codes:
@@ -264,19 +267,23 @@ def tile_wireless_power_allocation_s4_kernel(
         for k in range(NT):
             if k in VSQ:
                 square_v_mult(k)
+        mm1(4)
         square(0)
-        sat_tp = outs.tile([P, LOAD], F32, name="acc")
         sat_ps = satp.tile([P, LOAD], F32, name="sat_ps")
-        nc.tensor.transpose(sat_tp[:, 0:P], sat_w[:], ident[:])
-        nc.vector.tensor_copy(out=sat_t[:], in_=sat_tp[:, 0:P])
-        nc.tensor.transpose(sat_ps[:, 0:P], sat_t[:], ident[:])
+
+        def sat_to_psum():
+            sat_tp = outs.tile([P, LOAD], F32, name="acc")
+            nc.tensor.transpose(sat_tp[:, 0:P], sat_w[:], ident[:])
+            nc.vector.tensor_copy(out=sat_t[:], in_=sat_tp[:, 0:P])
+            nc.tensor.transpose(sat_ps[:, 0:P], sat_t[:], ident[:])
+
         v_early = {
             1: lambda: permute_codes(1, 0),
             2: lambda: permute_codes(1, 1),
             3: lambda: permute_scales(1),
-            6: lambda: permute_codes(2, 0),
-            7: lambda: permute_codes(2, 1),
-            10: lambda: permute_scales(2),
+            5: lambda: permute_codes(2, 0),
+            6: lambda: permute_codes(2, 1),
+            9: lambda: permute_scales(2),
         }
         fins = {}
         for k in range(n_steps - NT):
@@ -286,7 +293,13 @@ def tile_wireless_power_allocation_s4_kernel(
             if k + LEAD < n_steps:
                 mm1(k + LEAD)
             square(k + 1)
+            if k == 0:
+                nc.scalar.activation(
+                    out=neg_ton[:], in_=ton_b[:].rearrange("p g t -> p (g t)"), func=ACT.Copy, scale=-1.0
+                )
             sigmoid(k)
+            if k == SATK:
+                sat_to_psum()
             pu = u - 1
             done = pu in ends
             pc = ends[pu] if done else None
@@ -295,8 +308,10 @@ def tile_wireless_power_allocation_s4_kernel(
                     scale_by_sat(pu, 0, 512, GS)
             for f in fins.pop((u, j), []):
                 f()
-            if k + AHD in VSQ and k + AHD >= NT:
-                square_v_copy(k + AHD)
+            nxt = [x for x in VSQ if NT * (u + 1) <= x < NT * (u + 2)]
+            if j == CPJ:
+                for x in nxt:
+                    square_v_copy(x)
             if u >= 1 and j == 2:
                 quantize(pu, 0, 512)
                 if done:
@@ -308,8 +323,9 @@ def tile_wireless_power_allocation_s4_kernel(
                             if st < 2:
                                 mm2_all(c, st + 2)
                         fins.setdefault((u + du, fj), []).append(fin)
-            if k + 2 in VSQ and k + 2 >= NT:
-                square_v_mult(k + 2)
+            if j == MUJ:
+                for x in nxt:
+                    square_v_mult(x)
 
         k0 = n_steps - NT
         lc = NC - 1

@@ -25,7 +25,7 @@ NC = SLOT // C
 NT = 4
 
 LEAD = 5
-VSQ = [3, 9, 13, 17, 21, 25, 29, 37, 41]
+VSQ = [3, 9, 13, 17, 21, 25, 37, 41]
 CPJ = 1
 MUJ = 2
 SATK = 5
@@ -198,9 +198,9 @@ def tile_wireless_power_allocation_s4_kernel(
             g = order[u][1]
             n = c1 - c0
             eng.tensor_tensor(
-                out=h[:, NT * (c0 - base) : NT * (c1 - base)].rearrange("p (c i t) -> p c t i", i=2, t=NT),
-                in0=sig[u][:, :, c0:c1].rearrange("p t (c i) -> p c t i", i=2),
-                in1=factors[:, NT * g : NT * (g + 1)].unsqueeze(1).unsqueeze(3).broadcast_to([P, n // 2, NT, 2]),
+                out=h[:, NT * (c0 - base) : NT * (c1 - base)].rearrange("p (c i t) -> p c t i", i=4, t=NT),
+                in0=sig[u][:, :, c0:c1].rearrange("p t (c i) -> p c t i", i=4),
+                in1=factors[:, NT * g : NT * (g + 1)].unsqueeze(1).unsqueeze(3).broadcast_to([P, n // 4, NT, 4]),
                 op=ALU.mult,
             )
 

from contextlib import ExitStack

import concourse.mybir as mybir
from concourse.masks import make_identity

F32 = mybir.dt.float32
BF16 = mybir.dt.bfloat16
I32 = mybir.dt.int32
U32 = mybir.dt.uint32
U8 = mybir.dt.uint8
FP8X4 = mybir.dt.float8_e4m3fn_x4
FP4X4 = mybir.dt.float4_e2m1fn_x4
ACT = mybir.ActivationFunctionType
ALU = mybir.AluOpType

ANT, SLOT, DEV, LOAD = 1024, 2048, 1536, 512
FLOPS = 2 * ANT * SLOT * DEV + 2 * SLOT * DEV * LOAD

P = 128
K_PASS = 512
KP = ANT // K_PASS
NG = DEV // K_PASS
C = 512
NC = SLOT // C
NT = 4

LEAD = 5
VSQ = [3, 9, 13, 17, 21, 25, 37, 41]
CPJ = 1
MUJ = 2
SATK = 5
GU = 1
GS = 144
AMPS = 5
FSL = [(0, 3), (0, 3), (1, 1), (1, 3)]
SEGS = [(0, 256), (256, 384), (384, 512)]
AHD = 3


def tile_wireless_power_allocation_s4_kernel(
    tc, beam_words, beam_scales, chan_words, chan_scales, turn_on, sat, alloc_words, alloc_scales, out
):
    nc = tc.nc
    n_units = NC * NG
    n_steps = n_units * NT
    last = n_units - 1

    with ExitStack() as ctx:
        keep = ctx.enter_context(tc.tile_pool(name="keep", bufs=1))
        sqp = ctx.enter_context(tc.tile_pool(name="sqp", bufs=4))
        sigp = ctx.enter_context(tc.tile_pool(name="sigp", bufs=3))
        hbp = ctx.enter_context(tc.tile_pool(name="hbp", bufs=2))
        qp = ctx.enter_context(tc.tile_pool(name="qp", bufs=8))
        op = ctx.enter_context(tc.tile_pool(name="op", bufs=6))
        amps = ctx.enter_context(tc.psum_pool(name="amps", bufs=AMPS))
        satp = ctx.enter_context(tc.psum_pool(name="satp", bufs=1))
        outs = ctx.enter_context(tc.psum_pool(name="outs", bufs=2))
        ctx.enter_context(tc.manual_schedule())

        chan_raw0 = keep.tile([P, KP, 1024], U8, name="chan_raw0", align_bytes=64)
        chan_raw12 = keep.tile([P, KP, 2048], U8, name="chan_raw12", align_bytes=64)
        chan_sraw0 = keep.tile([P, KP, 512], U8, name="chan_sraw0", align_bytes=64)
        chan_sraw12 = keep.tile([P, KP, 1024], U8, name="chan_sraw12", align_bytes=64)
        chan_c = [keep.tile([P, NT, KP, 256], U8, name=f"chan_c{g}", align_bytes=64) for g in range(NG)]
        chan_s = [keep.tile([P, NT, KP, P], U8, name=f"chan_s{g}", align_bytes=64) for g in range(NG)]
        beam_c = [keep.tile([P, KP, 2 * C], U8, name=f"beam_c{c}", align_bytes=64) for c in range(NC)]
        beam_s0 = keep.tile([P, KP, C], U8, name="beam_s0", align_bytes=64)
        beam_s123 = keep.tile([P, KP, 3 * C], U8, name="beam_s123", align_bytes=64)
        alloc_c = keep.tile([P, NG, 4 * LOAD], U8, name="alloc_c", align_bytes=64)
        alloc_s = keep.tile([P, NG, LOAD], U8, name="alloc_s", align_bytes=64)
        ton_b = keep.tile([P, NG, NT], BF16, name="ton_b")
        sat_b = keep.tile([P, NG, NT], BF16, name="sat_b")
        neg_ton = keep.tile([P, NG * NT], F32, name="neg_ton")
        sat_w = keep.tile([P, P], F32, name="sat_w")
        sat_t = keep.tile([P, P], F32, name="sat_t")
        ident = keep.tile([P, P], F32, name="ident")
        dummy = keep.tile([P, 1], F32, name="dummy")
        dummy2 = keep.tile([P, 1], F32, name="dummy2")

        nc.vector.memset(chan_sraw0[:].bitcast(I32), 0)
        nc.vector.memset(beam_s0[:].bitcast(I32), 0)
        nc.vector.memset(dummy[:], 0.0)
        nc.vector.memset(sat_w[:], 0.0)
        nc.vector.memset(beam_s123[:].bitcast(I32), 0)
        nc.vector.memset(chan_sraw12[:].bitcast(I32), 0)
        nc.vector.memset(alloc_s[:].bitcast(I32), 0)

        cw = chan_words.bitcast(I32).rearrange("k p n -> p k n")
        bw = beam_words.bitcast(I32).rearrange("k p n -> p k n")
        cs = chan_scales.bitcast(I32).rearrange("k r n -> r k n")
        bs = beam_scales.bitcast(I32).rearrange("k r n -> r k n")
        als = alloc_scales.bitcast(I32).rearrange("k r n -> r k n")

        def load_scales(eng, tile, src, c0, c1, quarters=(0, 1, 2, 3)):
            view = tile[:].bitcast(I32)
            for q in quarters:
                eng.dma_start(out=view[32 * q : 32 * q + 4], in_=src[4 * q : 4 * q + 4, :, c0:c1])

        def load_beam(eng, c):
            eng.dma_start(out=beam_c[c][:].bitcast(I32), in_=bw[:, :, 256 * c : 256 * (c + 1)])

        load_beam(nc.gpsimd, 0)
        nc.sync.dma_start(out=chan_raw0[:].bitcast(I32), in_=cw[:, :, 0:256])
        load_scales(nc.scalar, chan_sraw0, cs, 0, 128)
        load_scales(nc.sync, beam_s0, bs, 0, 128, (0, 1, 2))
        load_scales(nc.gpsimd, beam_s0, bs, 0, 128, (3,))
        nc.gpsimd.dma_start(out=ton_b[:], in_=turn_on.rearrange("(g p t) -> p g t", g=NG, t=NT))
        nc.gpsimd.dma_start(out=sat_b[:], in_=sat.rearrange("(g p t) -> p g t", g=NG, t=NT))
        nc.scalar.activation(out=dummy2[:], in_=dummy[:], func=ACT.Sigmoid)
        nc.gpsimd.dma_start(out=chan_raw12[:].bitcast(I32), in_=cw[:, :, 256:768])
        load_scales(nc.sync, beam_s123, bs, 128, 512)
        load_beam(nc.sync, 1)
        load_scales(nc.sync, chan_sraw12, cs, 128, 384)
        nc.sync.dma_start(
            out=alloc_c[:].bitcast(I32),
            in_=alloc_words.rearrange("g p n t -> g p (n t)").bitcast(I32).rearrange("g p n -> p g n"),
        )
        load_scales(nc.sync, alloc_s, als, 0, 128)
        load_beam(nc.sync, 2)
        load_beam(nc.sync, 3)
        nc.gpsimd.tensor_copy(out=sat_w[:, 0 : NG * NT], in_=sat_b[:].rearrange("p g t -> p (g t)"))
        make_identity(nc, ident[:])

        def permute_first(t):
            nc.vector.tensor_copy(
                out=chan_c[0][:].rearrange("p t k (m b) -> p t k m b", b=2)[:, t],
                in_=chan_raw0[:].rearrange("p k (m t b) -> p t k m b", t=NT, b=2)[:, t],
            )
            nc.vector.tensor_copy(
                out=chan_s[0][:, t], in_=chan_sraw0[:].rearrange("p k (m t) -> p t k m", t=NT)[:, t]
            )

        def permute_codes(g, k):
            src = chan_raw12[:, :, 1024 * (g - 1) : 1024 * g]
            nc.vector.tensor_copy(
                out=chan_c[g][:].rearrange("p t k (m b) -> p k t m b", b=2)[:, k],
                in_=src.rearrange("p k (m t b) -> p k t m b", t=NT, b=2)[:, k],
            )

        def permute_scales(g):
            src = chan_sraw12[:, :, 512 * (g - 1) : 512 * g]
            nc.vector.tensor_copy(out=chan_s[g][:], in_=src.rearrange("p k (m t) -> p t k m", t=NT))

        order = [(0, 0), (1, 0), (0, 1), (1, 1), (0, 2), (1, 2)] + [(c, g) for c in (2, 3) for g in range(NG)]
        index = {cg: u for u, cg in enumerate(order)}
        ends = {index[c, NG - 1]: c for c in range(NC)}
        amp, sq, raw, sig, hb, codes, scales, acc = {}, {}, {}, {}, {}, {}, {}, {}

        def mm1(k):
            u, t = divmod(k, NT)
            c, g = order[u]
            a = amps.tile([P, C], F32, name="amp")
            amp[k] = a
            for kk in range(KP):
                if c == 0:
                    rs = beam_s0[:, kk, :]
                else:
                    rs = beam_s123[:, kk, C * (c - 1) : C * c]
                nc.tensor.matmul_mx(
                    out=a[:],
                    lhsT=chan_c[g][:, t, kk, :].bitcast(FP4X4),
                    lhsT_scale=chan_s[g][:, t, kk, :],
                    rhs=beam_c[c][:, kk, :].bitcast(FP4X4),
                    rhs_scale=rs,
                    start=(kk == 0),
                    stop=(kk == KP - 1),
                )

        def square_s(k):
            s = sqp.tile([P, C], F32, name="sq")
            sq[k] = s
            nc.scalar.activation(out=s[:], in_=amp[k][:], func=ACT.Square)

        def square_v_copy(k):
            r = sqp.tile([P, C], F32, name="raw")
            raw[k] = r
            nc.vector.tensor_copy(out=r[:], in_=amp[k][:])

        def square_v_mult(k):
            s = sqp.tile([P, C], F32, name="sq")
            sq[k] = s
            nc.vector.tensor_tensor(out=s[:], in0=raw[k][:], in1=raw[k][:], op=ALU.mult)

        def sigmoid(k, c0=0, c1=C):
            u, t = divmod(k, NT)
            g = order[u][1]
            if u not in sig:
                s = sigp.tile([P, NT, C], F32, name="sig")
                sig[u] = s
            nc.scalar.activation(
                out=sig[u][:, t, c0:c1],
                in_=sq[k][:, c0:c1],
                func=ACT.Sigmoid,
                bias=neg_ton[:, NT * g + t : NT * g + t + 1],
            )

        def scale_part(eng, u, h, base, c0, c1, factors):
            g = order[u][1]
            n = c1 - c0
            eng.tensor_tensor(
                out=h[:, NT * (c0 - base) : NT * (c1 - base)].rearrange("p (c i t) -> p c t i", i=4, t=NT),
                in0=sig[u][:, :, c0:c1].rearrange("p t (c i) -> p c t i", i=4),
                in1=factors[:, NT * g : NT * (g + 1)].unsqueeze(1).unsqueeze(3).broadcast_to([P, n // 4, NT, 4]),
                op=ALU.mult,
            )

        def scale_by_sat(u, c0, c1, share=0):
            h = hbp.tile([P, 4 * C], BF16, name="hb", align_bytes=64)
            hb[u, c0] = h
            if u < GU:
                share = 0
            if share:
                scale_part(nc.gpsimd, u, h, c0, c1 - share, c1, sat_w)
            scale_part(nc.vector, u, h, c0, c0, c1 - share, sat_ps if u >= GU else sat_w)

        def quantize(u, c0, c1):
            if u not in codes:
                qc = qp.tile([P, C], U32, name="qc", align_bytes=64)
                qs = qp.tile([P, C], U8, name="qs", align_bytes=64)
                codes[u] = qc
                scales[u] = qs
            nc.vector.quantize_mx(
                out=codes[u][:, c0:c1].bitcast(FP8X4),
                scales=scales[u][:, c0:c1],
                in_=hb[u, c0][:, 0 : NT * (c1 - c0)],
            )

        def mm2(c, st, g0, g1, a, n0=0, n1=LOAD):
            for g in range(g0, g1):
                u = index[c, g]
                nc.tensor.matmul_mx(
                    out=a[:, 0 : n1 - n0],
                    lhsT=codes[u][:, P * st : P * (st + 1)].bitcast(FP8X4),
                    lhsT_scale=scales[u][:, P * st : P * (st + 1)],
                    rhs=alloc_c[:, g, 4 * n0 : 4 * n1].bitcast(FP8X4),
                    rhs_scale=alloc_s[:, g, n0:n1],
                    start=(g == 0),
                    stop=(g == NG - 1),
                )

        def mm2_all(c, st):
            a = outs.tile([P, LOAD], F32, name="acc")
            acc[c, st] = a
            mm2(c, st, 0, NG, a)

        def finish(c, st, eng, a=None, n0=0, n1=LOAD, queue=None):
            a = acc[c, st] if a is None else a
            o = op.tile([P, LOAD], F32, name="o")
            w = n1 - n0
            if eng == "v":
                nc.vector.tensor_copy(out=o[:, 0:w], in_=a[:, 0:w])
            else:
                nc.scalar.copy(out=o[:, 0:w], in_=a[:, 0:w])
            row = C * c + P * st
            (queue or nc.sync).dma_start(out=out[row : row + P, n0:n1], in_=o[:, 0:w])

        def square(k):
            if k < n_steps and k not in VSQ:
                square_s(k)

        for t in range(NT):
            permute_first(t)
            mm1(t)
        for k in range(NT):
            if k in VSQ:
                square_v_copy(k)
        for k in range(NT):
            if k in VSQ:
                square_v_mult(k)
        mm1(4)
        square(0)
        sat_ps = satp.tile([P, LOAD], F32, name="sat_ps")

        def sat_to_psum():
            sat_tp = outs.tile([P, LOAD], F32, name="acc")
            nc.tensor.transpose(sat_tp[:, 0:P], sat_w[:], ident[:])
            nc.vector.tensor_copy(out=sat_t[:], in_=sat_tp[:, 0:P])
            nc.tensor.transpose(sat_ps[:, 0:P], sat_t[:], ident[:])

        v_early = {
            1: lambda: permute_codes(1, 0),
            2: lambda: permute_codes(1, 1),
            3: lambda: permute_scales(1),
            5: lambda: permute_codes(2, 0),
            6: lambda: permute_codes(2, 1),
            9: lambda: permute_scales(2),
        }
        fins = {}
        for k in range(n_steps - NT):
            u, j = divmod(k, NT)
            if k in v_early:
                v_early[k]()
            if k + LEAD < n_steps:
                mm1(k + LEAD)
            square(k + 1)
            if k == 0:
                nc.scalar.activation(
                    out=neg_ton[:], in_=ton_b[:].rearrange("p g t -> p (g t)"), func=ACT.Copy, scale=-1.0
                )
            sigmoid(k)
            if k == SATK:
                sat_to_psum()
            pu = u - 1
            done = pu in ends
            pc = ends[pu] if done else None
            if u >= 1:
                if j == 0:
                    scale_by_sat(pu, 0, 512, GS)
            for f in fins.pop((u, j), []):
                f()
            nxt = [x for x in VSQ if NT * (u + 1) <= x < NT * (u + 2)]
            if j == CPJ:
                for x in nxt:
                    square_v_copy(x)
            if u >= 1 and j == 2:
                quantize(pu, 0, 512)
                if done:
                    mm2_all(pc, 0)
                    mm2_all(pc, 1)
                    for st, (du, fj) in enumerate(FSL):
                        def fin(c=pc, st=st):
                            finish(c, st, "v")
                            if st < 2:
                                mm2_all(c, st + 2)
                        fins.setdefault((u + du, fj), []).append(fin)
            if j == MUJ:
                for x in nxt:
                    square_v_mult(x)

        k0 = n_steps - NT
        lc = NC - 1
        segs = SEGS
        pu = last - 1
        square(k0 + 1)
        square(k0 + 2)
        square(k0 + 3)
        scale_by_sat(pu, 0, 512, GS)
        for key in sorted(fins):
            for f in fins[key]:
                f()
        quantize(pu, 0, 512)
        final = {}
        for key in ("0", "1", "2", "3a", "3b"):
            a = amps.tile([P, C], F32, name="amp")
            final[key] = a
        parts = [("0", 0, 0, 512), ("1", 1, 0, 512), ("2", 2, 0, 512), ("3a", 3, 0, 256), ("3b", 3, 256, 512)]
        for key, s, n0, n1 in parts:
            mm2(lc, s, 0, NG - 1, final[key], n0, n1)
        for c0, c1 in segs:
            for t in range(NT):
                sigmoid(k0 + t, c0, c1)
        for i, (c0, c1) in enumerate(segs):
            scale_by_sat(last, c0, c1)
            if i > 0:
                quantize(last, *segs[i - 1])
        quantize(last, *segs[-1])
        for key, s, n0, n1 in parts:
            mm2(lc, s, NG - 1, NG, final[key], n0, n1)
        finish(lc, 0, "s", final["0"])
        finish(lc, 1, "s", final["1"])
        finish(lc, 2, "v", final["2"])
        finish(lc, 3, "s", final["3a"], 0, 256, nc.scalar)
        finish(lc, 3, "v", final["3b"], 256, 512)
